import numpy as np
import ml_dtypes


def mxq(x, axis, fmt="e4m3"):
    dtype, down = {"e4m3": (ml_dtypes.float8_e4m3fn, 7), "e5m2": (ml_dtypes.float8_e5m2, 14)}[fmt]
    v = np.moveaxis(np.asarray(x, np.float32).astype(ml_dtypes.bfloat16).astype(np.float64), axis, -1)
    blocks = v.reshape(v.shape[:-1] + (-1, 32))
    amax = np.abs(blocks).max(-1, keepdims=True)
    byte = np.maximum(np.where(amax > 0, np.frexp(amax)[1] - 1 + 127, 0) - down, 1)
    scale = np.exp2(byte - 127.0)
    codes = (blocks / scale).astype(np.float32).astype(dtype).astype(np.float64)
    return np.moveaxis((codes * scale).reshape(v.shape), -1, axis)


WIDE = False


def mx_kscale(k):
    if not WIDE:
        return np.ones(k)
    levels = np.array([30, -30])
    if k % 512:
        return np.exp2(np.random.permutation(np.resize(levels, k // 32))).repeat(32)
    a = np.empty((k // 512, 16))
    for p in range(k // 512):
        a[p, :8] = np.random.permutation(np.resize(levels, 8))
        for g in range(8):
            far = levels[np.abs(levels - a[p, g]) >= 10]
            a[p, g + 8] = far[np.random.randint(len(far))]
    return np.exp2(a.ravel()).repeat(32)


def f64(x):
    return np.asarray(x).astype(np.float64)


T, D, H = 3072, 640, 512


def setup_inputs():
    n = np.random.standard_normal
    s1 = mx_kscale(T)[:, None]
    s2 = mx_kscale(T)[:, None]
    m = np.exp(0.5 * n((T, 1)))
    return {
        "x": (n((T, D)) * s1).astype(np.float32),
        "de": (m * n((T, H)) / np.sqrt(T) / s1).astype(np.float32),
        "dr": (m * n((T, D)) / np.sqrt(T) * s2).astype(np.float32),
        "e": (n((T, H)) / s2).astype(np.float32),
        "p": (0.1 * n((640, 512))).astype(np.float32),
    }


def reference(x, de, dr, e, p):
    x_ = mxq(f64(x), 0, "e4m3")
    de_ = mxq(f64(de), 0, "e5m2")
    dr_ = mxq(f64(dr), 0, "e5m2")
    e_ = mxq(f64(e), 0, "e4m3")
    y = x_.T @ de_ + dr_.T @ e_
    return f64(p) - 0.0625 * y

@@ -1,0 +1,160 @@
+from contextlib import ExitStack
+
+import concourse.mybir as mybir
+
+T, D, H = 3072, 640, 512
+LEARNING_RATE = 0.0625
+
+FLOPS = 4 * T * D * H
+
+F32 = mybir.dt.float32
+BF16 = mybir.dt.bfloat16
+U32 = mybir.dt.uint32
+U8 = mybir.dt.uint8
+E4M3 = mybir.dt.float8_e4m3fn_x4
+E5M2 = mybir.dt.float8_e5m2_x4
+MULT = mybir.AluOpType.mult
+ADD = mybir.AluOpType.add
+
+P = 128
+PACK = 4
+T_PASS = P * PACK
+PASSES = T // T_PASS
+D_TILE = 128
+D_TILES = D // D_TILE
+VECTOR_SHARE = 320
+GROUPS = [(0, 2), (2, 2), (4, 1)]
+MAIN = 512
+
+
+def tile_mix_tied_sgd_kernel(tc, x, de, dr, e, p, out):
+    nc = tc.nc
+
+    with ExitStack() as ctx:
+        raw = ctx.enter_context(tc.tile_pool(name="raw", bufs=3))
+        grouped = ctx.enter_context(tc.tile_pool(name="grouped", bufs=3))
+        packed = ctx.enter_context(tc.tile_pool(name="packed", bufs=4))
+        keep = ctx.enter_context(tc.tile_pool(name="keep", bufs=1))
+        psum = ctx.enter_context(tc.psum_pool(name="psum", bufs=1))
+        ctx.enter_context(tc.manual_schedule())
+
+        acc = [psum.tile([P, H], F32, name=f"acc{b}") for b in range(D_TILES)]
+
+        def load(pool, tag, source, first, count, cols):
+            rows = pool.tile([P, count, PACK, cols.stop - cols.start], F32, name=tag)
+            nc.sync.dma_start(
+                out=rows[:],
+                in_=source[first * T_PASS : (first + count) * T_PASS, cols].rearrange(
+                    "(g q j) w -> q g j w", g=count, j=PACK
+                ),
+            )
+            return rows
+
+        def interleave(copy, grp, grp_cols, rows):
+            copy(out=grp[:, grp_cols, :], in_=rows.rearrange("q j w -> q w j"))
+
+        def quantize(op, cols):
+            grp, codes, scales, fmt = op
+            nc.vector.quantize_mx(
+                out=codes[:, cols].bitcast(fmt),
+                scales=scales[:, cols],
+                in_=grp[:, cols, :].rearrange("q w j -> q (w j)"),
+            )
+
+        def multiply(b, wide, narrow, start, stop):
+            cols = slice(b * D_TILE, (b + 1) * D_TILE)
+            nc.tensor.matmul_mx(
+                out=acc[b][:],
+                lhsT=wide[1][:, cols].bitcast(wide[3]),
+                lhsT_scale=wide[2][:, cols],
+                rhs=narrow[1][:].bitcast(narrow[3]),
+                rhs_scale=narrow[2][:],
+                start=start,
+                stop=stop,
+            )
+
+        def operand(tag, width, fmt):
+            grp = grouped.tile([P, width, PACK], BF16, name=tag + "_grp", align_bytes=64)
+            codes = packed.tile([P, width], U32, name=tag + "_codes", align_bytes=64)
+            scales = packed.tile([P, width], U8, name=tag + "_scales", align_bytes=64)
+            return grp, codes, scales, fmt
+
+        tiles = [slice(b * D_TILE, (b + 1) * D_TILE) for b in range(D_TILES)]
+        main = slice(0, MAIN)
+        rest = slice(MAIN, D)
+        lower = slice(0, VECTOR_SHARE)
+        upper = slice(VECTOR_SHARE, H)
+
+        for first, count in GROUPS:
+            for wide_src, wide_fmt, narrow_src, narrow_fmt in ((x, E4M3, de, E5M2), (dr, E5M2, e, E4M3)):
+                n_raw = load(raw, "narrow_raw", narrow_src, first, count, slice(0, H))
+                w_raw = load(raw, "wide_raw", wide_src, first, count, slice(0, D))
+                for g in range(count):
+                    narrow = operand("narrow", H, narrow_fmt)
+                    wide = operand("wide", D, wide_fmt)
+                    interleave(nc.scalar.copy, narrow[0], slice(0, H), n_raw[:, g])
+                    interleave(nc.scalar.copy, wide[0], rest, w_raw[:, g, :, rest])
+                    interleave(nc.vector.tensor_copy, wide[0], main, w_raw[:, g, :, main])
+                    quantize(narrow, slice(0, H))
+                    quantize(wide, main)
+                    quantize(wide, rest)
+                    for b in range(D_TILES):
+                        multiply(b, wide, narrow, first + g == 0 and wide_src is x, False)
+
+        k = PASSES - 1
+        x_raw = load(keep, "x_raw", x, k, 1, slice(0, D))
+        de_raw = load(keep, "de_raw", de, k, 1, slice(0, H))
+        e_raw = load(keep, "e_raw", e, k, 1, slice(0, H))
+        dra_raw = load(keep, "dra_raw", dr, k, 1, main)
+        p_rows = p.rearrange("(b q) h -> q b h", q=P)
+        o_rows = out.rearrange("(b q) h -> q b h", q=P)
+        p_sb = keep.tile([P, D_TILES, H], F32, name="p_sb")
+
+        def load_p(lo, hi):
+            nc.sync.dma_start(out=p_sb[:, lo:hi, :], in_=p_rows[:, lo:hi, :])
+
+        load_p(0, 2)
+        drb_raw = load(keep, "drb_raw", dr, k, 1, rest)
+        load_p(2, 4)
+        load_p(4, 5)
+
+        x_op = operand("wide", D, E4M3)
+        de_op = operand("narrow", H, E5M2)
+        e_op = operand("narrow", H, E4M3)
+        dr_op = operand("wide", D, E5M2)
+
+        interleave(nc.scalar.copy, x_op[0], rest, x_raw[:, 0, :, rest])
+        interleave(nc.vector.tensor_copy, x_op[0], main, x_raw[:, 0, :, main])
+        quantize(x_op, rest)
+        quantize(x_op, main)
+        interleave(nc.scalar.copy, de_op[0], upper, de_raw[:, 0, :, upper])
+        interleave(nc.vector.tensor_copy, de_op[0], lower, de_raw[:, 0, :, lower])
+        quantize(de_op, slice(0, H))
+        for b in range(D_TILES):
+            multiply(b, x_op, de_op, False, False)
+
+        def update(b):
+            result = keep.tile([P, H], F32, name=f"result{b}")
+            nc.vector.scalar_tensor_tensor(
+                out=result[:], in0=acc[b][:], scalar=-LEARNING_RATE, in1=p_sb[:, b, :], op0=MULT, op1=ADD
+            )
+            nc.sync.dma_start(out=o_rows[:, b, :], in_=result[:])
+
+        interleave(nc.vector.tensor_copy, e_op[0], lower, e_raw[:, 0, :, lower])
+        interleave(nc.scalar.copy, e_op[0], upper, e_raw[:, 0, :, upper])
+        quantize(e_op, slice(0, H))
+        interleave(nc.vector.tensor_copy, dr_op[0], tiles[0], dra_raw[:, 0, :, tiles[0]])
+        interleave(nc.scalar.copy, dr_op[0], tiles[1], dra_raw[:, 0, :, tiles[1]])
+        interleave(nc.vector.tensor_copy, dr_op[0], tiles[2], dra_raw[:, 0, :, tiles[2]])
+        interleave(nc.scalar.copy, dr_op[0], tiles[3], dra_raw[:, 0, :, tiles[3]])
+        interleave(nc.scalar.copy, dr_op[0], rest, drb_raw[:, 0])
+        for b in range(4):
+            quantize(dr_op, tiles[b])
+            multiply(b, dr_op, e_op, False, True)
+        update(0)
+        update(1)
+        quantize(dr_op, rest)
+        multiply(4, dr_op, e_op, False, True)
+        update(2)
+        update(3)
+        update(4)

@@ -25,6 +25,7 @@ D_TILES = D // D_TILE
 VECTOR_SHARE = 320
 GROUPS = [(0, 2), (2, 2), (4, 1)]
 MAIN = 512
+EARLY = 3
 
 
 def tile_mix_tied_sgd_kernel(tc, x, de, dr, e, p, out):
@@ -105,7 +106,6 @@ def tile_mix_tied_sgd_kernel(tc, x, de, dr, e, p, out):
         x_raw = load(keep, "x_raw", x, k, 1, slice(0, D))
         de_raw = load(keep, "de_raw", de, k, 1, slice(0, H))
         e_raw = load(keep, "e_raw", e, k, 1, slice(0, H))
-        dra_raw = load(keep, "dra_raw", dr, k, 1, main)
         p_rows = p.rearrange("(b q) h -> q b h", q=P)
         o_rows = out.rearrange("(b q) h -> q b h", q=P)
         p_sb = keep.tile([P, D_TILES, H], F32, name="p_sb")
@@ -113,10 +113,10 @@ def tile_mix_tied_sgd_kernel(tc, x, de, dr, e, p, out):
         def load_p(lo, hi):
             nc.sync.dma_start(out=p_sb[:, lo:hi, :], in_=p_rows[:, lo:hi, :])
 
-        load_p(0, 2)
-        drb_raw = load(keep, "drb_raw", dr, k, 1, rest)
-        load_p(2, 4)
-        load_p(4, 5)
+        dra_raw = load(keep, "dra_raw", dr, k, 1, slice(0, EARLY * D_TILE))
+        drb_raw = load(keep, "drb_raw", dr, k, 1, slice(EARLY * D_TILE, D))
+        for b in range(D_TILES):
+            load_p(b, b + 1)
 
         x_op = operand("wide", D, E4M3)
         de_op = operand("narrow", H, E5M2)
@@ -143,18 +143,24 @@ def tile_mix_tied_sgd_kernel(tc, x, de, dr, e, p, out):
         interleave(nc.vector.tensor_copy, e_op[0], lower, e_raw[:, 0, :, lower])
         interleave(nc.scalar.copy, e_op[0], upper, e_raw[:, 0, :, upper])
         quantize(e_op, slice(0, H))
-        interleave(nc.vector.tensor_copy, dr_op[0], tiles[0], dra_raw[:, 0, :, tiles[0]])
-        interleave(nc.scalar.copy, dr_op[0], tiles[1], dra_raw[:, 0, :, tiles[1]])
-        interleave(nc.vector.tensor_copy, dr_op[0], tiles[2], dra_raw[:, 0, :, tiles[2]])
-        interleave(nc.scalar.copy, dr_op[0], tiles[3], dra_raw[:, 0, :, tiles[3]])
-        interleave(nc.scalar.copy, dr_op[0], rest, drb_raw[:, 0])
-        for b in range(4):
+        def round_tile(copy, b, rows, first_tile):
+            interleave(copy, dr_op[0], tiles[b], rows[:, 0, :, tiles[b - first_tile]])
+
+        def close(b):
             quantize(dr_op, tiles[b])
             multiply(b, dr_op, e_op, False, True)
+
+        round_tile(nc.vector.tensor_copy, 0, dra_raw, 0)
+        round_tile(nc.scalar.copy, 1, dra_raw, 0)
+        round_tile(nc.vector.tensor_copy, 2, dra_raw, 0)
+        round_tile(nc.scalar.copy, 3, drb_raw, EARLY)
+        round_tile(nc.scalar.copy, 4, drb_raw, EARLY)
+        for b in range(EARLY):
+            close(b)
         update(0)
+        close(3)
         update(1)
-        quantize(dr_op, rest)
-        multiply(4, dr_op, e_op, False, True)
+        close(4)
         update(2)
         update(3)
         update(4)

@@ -23,7 +23,10 @@ PASSES = T // T_PASS
 D_TILE = 128
 D_TILES = D // D_TILE
 VECTOR_SHARE = 320
-GROUPS = [(0, 2), (2, 2), (4, 1)]
+GROUPS = [(0, 3), (3, 2)]
+WIDE_SHARE = 384
+NARROW_SHARE = 272
+WIDEST = 1024
 MAIN = 512
 EARLY = 3
 
@@ -32,9 +35,9 @@ def tile_mix_tied_sgd_kernel(tc, x, de, dr, e, p, out):
     nc = tc.nc
 
     with ExitStack() as ctx:
-        raw = ctx.enter_context(tc.tile_pool(name="raw", bufs=3))
-        grouped = ctx.enter_context(tc.tile_pool(name="grouped", bufs=3))
-        packed = ctx.enter_context(tc.tile_pool(name="packed", bufs=4))
+        raw = ctx.enter_context(tc.tile_pool(name="raw", bufs=2))
+        grouped = ctx.enter_context(tc.tile_pool(name="grouped", bufs=2))
+        packed = ctx.enter_context(tc.tile_pool(name="packed", bufs=2))
         keep = ctx.enter_context(tc.tile_pool(name="keep", bufs=1))
         psum = ctx.enter_context(tc.psum_pool(name="psum", bufs=1))
         ctx.enter_context(tc.manual_schedule())
@@ -62,14 +65,35 @@ def tile_mix_tied_sgd_kernel(tc, x, de, dr, e, p, out):
                 in_=grp[:, cols, :].rearrange("q w j -> q (w j)"),
             )
 
-        def multiply(b, wide, narrow, start, stop):
-            cols = slice(b * D_TILE, (b + 1) * D_TILE)
+        def quantize_all(op, width):
+            done = 0
+            step = WIDEST
+            while done < width:
+                if done + step <= width:
+                    quantize(op, slice(done, done + step))
+                    done = done + step
+                else:
+                    step = step // 2
+
+        def round_shared(op, rows, count, share, width):
+            for g in range(count):
+                interleave(nc.scalar.copy, op[0], slice(g * width + share, (g + 1) * width), rows[:, g, :, share:width])
+            nc.vector.tensor_copy(
+                out=op[0][:].rearrange("q (g w) j -> q g w j", g=count)[:, :, 0:share, :].rearrange(
+                    "q g (u w) j -> q u g w j", u=2
+                ),
+                in_=rows[:, :, :, 0:share].rearrange("q g j (u w) -> q u g w j", u=2),
+            )
+
+        def multiply(b, wide, narrow, start, stop, g=0):
+            cols = slice(g * D + b * D_TILE, g * D + (b + 1) * D_TILE)
+            moving = slice(g * H, (g + 1) * H)
             nc.tensor.matmul_mx(
                 out=acc[b][:],
                 lhsT=wide[1][:, cols].bitcast(wide[3]),
                 lhsT_scale=wide[2][:, cols],
-                rhs=narrow[1][:].bitcast(narrow[3]),
-                rhs_scale=narrow[2][:],
+                rhs=narrow[1][:, moving].bitcast(narrow[3]),
+                rhs_scale=narrow[2][:, moving],
                 start=start,
                 stop=stop,
             )
@@ -90,22 +114,20 @@ def tile_mix_tied_sgd_kernel(tc, x, de, dr, e, p, out):
             for wide_src, wide_fmt, narrow_src, narrow_fmt in ((x, E4M3, de, E5M2), (dr, E5M2, e, E4M3)):
                 n_raw = load(raw, "narrow_raw", narrow_src, first, count, slice(0, H))
                 w_raw = load(raw, "wide_raw", wide_src, first, count, slice(0, D))
+                narrow = operand("narrow", count * H, narrow_fmt)
+                wide = operand("wide", count * D, wide_fmt)
+                round_shared(narrow, n_raw, count, NARROW_SHARE, H)
+                quantize_all(narrow, count * H)
+                round_shared(wide, w_raw, count, WIDE_SHARE, D)
+                quantize_all(wide, count * D)
                 for g in range(count):
-                    narrow = operand("narrow", H, narrow_fmt)
-                    wide = operand("wide", D, wide_fmt)
-                    interleave(nc.scalar.copy, narrow[0], slice(0, H), n_raw[:, g])
-                    interleave(nc.scalar.copy, wide[0], rest, w_raw[:, g, :, rest])
-                    interleave(nc.vector.tensor_copy, wide[0], main, w_raw[:, g, :, main])
-                    quantize(narrow, slice(0, H))
-                    quantize(wide, main)
-                    quantize(wide, rest)
                     for b in range(D_TILES):
-                        multiply(b, wide, narrow, first + g == 0 and wide_src is x, False)
+                        multiply(b, wide, narrow, first + g == 0 and wide_src is x, False, g)
 
         k = PASSES - 1
-        x_raw = load(keep, "x_raw", x, k, 1, slice(0, D))
-        de_raw = load(keep, "de_raw", de, k, 1, slice(0, H))
-        e_raw = load(keep, "e_raw", e, k, 1, slice(0, H))
+        x_raw = load(raw, "wide_raw", x, k, 1, slice(0, D))
+        de_raw = load(raw, "narrow_raw", de, k, 1, slice(0, H))
+        e_raw = load(raw, "narrow_raw", e, k, 1, slice(0, H))
         p_rows = p.rearrange("(b q) h -> q b h", q=P)
         o_rows = out.rearrange("(b q) h -> q b h", q=P)
         p_sb = keep.tile([P, D_TILES, H], F32, name="p_sb")
@@ -123,12 +145,10 @@ def tile_mix_tied_sgd_kernel(tc, x, de, dr, e, p, out):
         e_op = operand("narrow", H, E4M3)
         dr_op = operand("wide", D, E5M2)
 
-        interleave(nc.scalar.copy, x_op[0], rest, x_raw[:, 0, :, rest])
-        interleave(nc.vector.tensor_copy, x_op[0], main, x_raw[:, 0, :, main])
-        quantize(x_op, rest)
+        round_shared(x_op, x_raw, 1, D // 2, D)
         quantize(x_op, main)
-        interleave(nc.scalar.copy, de_op[0], upper, de_raw[:, 0, :, upper])
-        interleave(nc.vector.tensor_copy, de_op[0], lower, de_raw[:, 0, :, lower])
+        quantize(x_op, rest)
+        round_shared(de_op, de_raw, 1, H // 2, H)
         quantize(de_op, slice(0, H))
         for b in range(D_TILES):
             multiply(b, x_op, de_op, False, False)

@@ -22,13 +22,15 @@ T_PASS = P * PACK
 PASSES = T // T_PASS
 D_TILE = 128
 D_TILES = D // D_TILE
-VECTOR_SHARE = 320
+
 GROUPS = [(0, 3), (3, 2)]
+LAST = PASSES - 1
 WIDE_SHARE = 384
 NARROW_SHARE = 272
-WIDEST = 1024
-MAIN = 512
+LAST_SHARE = 320
 EARLY = 3
+WIDEST = 1024
+RUN = 2
 
 
 def tile_mix_tied_sgd_kernel(tc, x, de, dr, e, p, out):
@@ -54,8 +56,11 @@ def tile_mix_tied_sgd_kernel(tc, x, de, dr, e, p, out):
             )
             return rows
 
-        def interleave(copy, grp, grp_cols, rows):
-            copy(out=grp[:, grp_cols, :], in_=rows.rearrange("q j w -> q w j"))
+        def interleave(copy, op, cols, rows):
+            copy(
+                out=op[0][:, cols, :].rearrange("q (c i) j -> q c j i", i=RUN),
+                in_=rows.rearrange("q j (c i) -> q c j i", i=RUN),
+            )
 
         def quantize(op, cols):
             grp, codes, scales, fmt = op
@@ -65,27 +70,40 @@ def tile_mix_tied_sgd_kernel(tc, x, de, dr, e, p, out):
                 in_=grp[:, cols, :].rearrange("q w j -> q (w j)"),
             )
 
-        def quantize_all(op, width):
+        def operand(tag, width, fmt):
+            grp = grouped.tile([P, width, PACK], BF16, name=tag + "_grp", align_bytes=64)
+            codes = packed.tile([P, width], U32, name=tag + "_codes", align_bytes=64)
+            scales = packed.tile([P, width], U8, name=tag + "_scales", align_bytes=64)
+            return grp, codes, scales, fmt
+
+        def prepare(tag, source, fmt, first, count, share):
+            width = source.shape[1]
+            rows = load(raw, tag + "_raw", source, first, count, slice(0, width))
+            op = operand(tag, count * width, fmt)
+            for g in range(count):
+                interleave(nc.scalar.copy, op, slice(g * width + share, (g + 1) * width), rows[:, g, :, share:width])
+            target = op[0][:].rearrange("q (g w) j -> q g w j", g=count)[:, :, 0:share, :]
+            if count == 1 or count % 2 == 0:
+                nc.vector.tensor_copy(
+                    out=target.rearrange("q g (c i) j -> q g c j i", i=RUN),
+                    in_=rows[:, :, :, 0:share].rearrange("q g j (c i) -> q g c j i", i=RUN),
+                )
+            else:
+                nc.vector.tensor_copy(
+                    out=target.rearrange("q g (u w) j -> q u g w j", u=2),
+                    in_=rows[:, :, :, 0:share].rearrange("q g j (u w) -> q u g w j", u=2),
+                )
             done = 0
             step = WIDEST
-            while done < width:
-                if done + step <= width:
+            while done < count * width:
+                if done + step <= count * width:
                     quantize(op, slice(done, done + step))
                     done = done + step
                 else:
                     step = step // 2
+            return op
 
-        def round_shared(op, rows, count, share, width):
-            for g in range(count):
-                interleave(nc.scalar.copy, op[0], slice(g * width + share, (g + 1) * width), rows[:, g, :, share:width])
-            nc.vector.tensor_copy(
-                out=op[0][:].rearrange("q (g w) j -> q g w j", g=count)[:, :, 0:share, :].rearrange(
-                    "q g (u w) j -> q u g w j", u=2
-                ),
-                in_=rows[:, :, :, 0:share].rearrange("q g j (u w) -> q u g w j", u=2),
-            )
-
-        def multiply(b, wide, narrow, start, stop, g=0):
+        def multiply(b, wide, narrow, g, start, stop):
             cols = slice(g * D + b * D_TILE, g * D + (b + 1) * D_TILE)
             moving = slice(g * H, (g + 1) * H)
             nc.tensor.matmul_mx(
@@ -98,60 +116,39 @@ def tile_mix_tied_sgd_kernel(tc, x, de, dr, e, p, out):
                 stop=stop,
             )
 
-        def operand(tag, width, fmt):
-            grp = grouped.tile([P, width, PACK], BF16, name=tag + "_grp", align_bytes=64)
-            codes = packed.tile([P, width], U32, name=tag + "_codes", align_bytes=64)
-            scales = packed.tile([P, width], U8, name=tag + "_scales", align_bytes=64)
-            return grp, codes, scales, fmt
-
-        tiles = [slice(b * D_TILE, (b + 1) * D_TILE) for b in range(D_TILES)]
-        main = slice(0, MAIN)
-        rest = slice(MAIN, D)
-        lower = slice(0, VECTOR_SHARE)
-        upper = slice(VECTOR_SHARE, H)
-
         for first, count in GROUPS:
             for wide_src, wide_fmt, narrow_src, narrow_fmt in ((x, E4M3, de, E5M2), (dr, E5M2, e, E4M3)):
-                n_raw = load(raw, "narrow_raw", narrow_src, first, count, slice(0, H))
-                w_raw = load(raw, "wide_raw", wide_src, first, count, slice(0, D))
-                narrow = operand("narrow", count * H, narrow_fmt)
-                wide = operand("wide", count * D, wide_fmt)
-                round_shared(narrow, n_raw, count, NARROW_SHARE, H)
-                quantize_all(narrow, count * H)
-                round_shared(wide, w_raw, count, WIDE_SHARE, D)
-                quantize_all(wide, count * D)
+                narrow = prepare("narrow", narrow_src, narrow_fmt, first, count, NARROW_SHARE)
+                wide = prepare("wide", wide_src, wide_fmt, first, count, WIDE_SHARE)
                 for g in range(count):
                     for b in range(D_TILES):
-                        multiply(b, wide, narrow, first + g == 0 and wide_src is x, False, g)
+                        multiply(b, wide, narrow, g, first + g == 0 and wide_src is x, False)
 
-        k = PASSES - 1
-        x_raw = load(raw, "wide_raw", x, k, 1, slice(0, D))
-        de_raw = load(raw, "narrow_raw", de, k, 1, slice(0, H))
-        e_raw = load(raw, "narrow_raw", e, k, 1, slice(0, H))
+        x_op = prepare("wide", x, E4M3, LAST, 1, WIDE_SHARE)
+        de_op = prepare("narrow", de, E5M2, LAST, 1, NARROW_SHARE)
+        for b in range(D_TILES):
+            multiply(b, x_op, de_op, 0, False, False)
+        e_op = prepare("narrow", e, E4M3, LAST, 1, LAST_SHARE)
+
+        early = load(keep, "early", dr, LAST, 1, slice(0, EARLY * D_TILE))
+        late = load(keep, "late", dr, LAST, 1, slice(EARLY * D_TILE, D))
         p_rows = p.rearrange("(b q) h -> q b h", q=P)
         o_rows = out.rearrange("(b q) h -> q b h", q=P)
         p_sb = keep.tile([P, D_TILES, H], F32, name="p_sb")
-
-        def load_p(lo, hi):
-            nc.sync.dma_start(out=p_sb[:, lo:hi, :], in_=p_rows[:, lo:hi, :])
-
-        dra_raw = load(keep, "dra_raw", dr, k, 1, slice(0, EARLY * D_TILE))
-        drb_raw = load(keep, "drb_raw", dr, k, 1, slice(EARLY * D_TILE, D))
         for b in range(D_TILES):
-            load_p(b, b + 1)
+            nc.sync.dma_start(out=p_sb[:, b : b + 1, :], in_=p_rows[:, b : b + 1, :])
 
-        x_op = operand("wide", D, E4M3)
-        de_op = operand("narrow", H, E5M2)
-        e_op = operand("narrow", H, E4M3)
         dr_op = operand("wide", D, E5M2)
 
-        round_shared(x_op, x_raw, 1, D // 2, D)
-        quantize(x_op, main)
-        quantize(x_op, rest)
-        round_shared(de_op, de_raw, 1, H // 2, H)
-        quantize(de_op, slice(0, H))
-        for b in range(D_TILES):
-            multiply(b, x_op, de_op, False, False)
+        def round_tile(copy, b):
+            rows, place = (early, b) if b < EARLY else (late, b - EARLY)
+            interleave(
+                copy, dr_op, slice(b * D_TILE, (b + 1) * D_TILE), rows[:, 0, :, place * D_TILE : (place + 1) * D_TILE]
+            )
+
+        def close(b):
+            quantize(dr_op, slice(b * D_TILE, (b + 1) * D_TILE))
+            multiply(b, dr_op, e_op, 0, False, True)
 
         def update(b):
             result = keep.tile([P, H], F32, name=f"result{b}")
@@ -160,23 +157,14 @@ def tile_mix_tied_sgd_kernel(tc, x, de, dr, e, p, out):
             )
             nc.sync.dma_start(out=o_rows[:, b, :], in_=result[:])
 
-        interleave(nc.vector.tensor_copy, e_op[0], lower, e_raw[:, 0, :, lower])
-        interleave(nc.scalar.copy, e_op[0], upper, e_raw[:, 0, :, upper])
-        quantize(e_op, slice(0, H))
-        def round_tile(copy, b, rows, first_tile):
-            interleave(copy, dr_op[0], tiles[b], rows[:, 0, :, tiles[b - first_tile]])
-
-        def close(b):
-            quantize(dr_op, tiles[b])
-            multiply(b, dr_op, e_op, False, True)
-
-        round_tile(nc.vector.tensor_copy, 0, dra_raw, 0)
-        round_tile(nc.scalar.copy, 1, dra_raw, 0)
-        round_tile(nc.vector.tensor_copy, 2, dra_raw, 0)
-        round_tile(nc.scalar.copy, 3, drb_raw, EARLY)
-        round_tile(nc.scalar.copy, 4, drb_raw, EARLY)
-        for b in range(EARLY):
-            close(b)
+        round_tile(nc.vector.tensor_copy, 0)
+        round_tile(nc.scalar.copy, 1)
+        close(0)
+        round_tile(nc.vector.tensor_copy, 2)
+        round_tile(nc.scalar.copy, 3)
+        round_tile(nc.scalar.copy, 4)
+        close(1)
+        close(2)
         update(0)
         close(3)
         update(1)

@@ -56,6 +56,12 @@ def tile_mix_tied_sgd_kernel(tc, x, de, dr, e, p, out):
             )
             return rows
 
+        def operand(tag, width, fmt):
+            values = grouped.tile([P, width, PACK], BF16, name=tag + "_grp", align_bytes=64)
+            codes = packed.tile([P, width], U32, name=tag + "_codes", align_bytes=64)
+            scales = packed.tile([P, width], U8, name=tag + "_scales", align_bytes=64)
+            return values, codes, scales, fmt
+
         def interleave(copy, op, cols, rows):
             copy(
                 out=op[0][:, cols, :].rearrange("q (c i) j -> q c j i", i=RUN),
@@ -63,18 +69,12 @@ def tile_mix_tied_sgd_kernel(tc, x, de, dr, e, p, out):
             )
 
         def quantize(op, cols):
-            grp, codes, scales, fmt = op
+            values, codes, scales, fmt = op
             nc.vector.quantize_mx(
                 out=codes[:, cols].bitcast(fmt),
                 scales=scales[:, cols],
-                in_=grp[:, cols, :].rearrange("q w j -> q (w j)"),
+                in_=values[:, cols, :].rearrange("q w j -> q (w j)"),
             )
-
-        def operand(tag, width, fmt):
-            grp = grouped.tile([P, width, PACK], BF16, name=tag + "_grp", align_bytes=64)
-            codes = packed.tile([P, width], U32, name=tag + "_codes", align_bytes=64)
-            scales = packed.tile([P, width], U8, name=tag + "_scales", align_bytes=64)
-            return grp, codes, scales, fmt
 
         def prepare(tag, source, fmt, first, count, share):
             width = source.shape[1]
@@ -83,16 +83,10 @@ def tile_mix_tied_sgd_kernel(tc, x, de, dr, e, p, out):
             for g in range(count):
                 interleave(nc.scalar.copy, op, slice(g * width + share, (g + 1) * width), rows[:, g, :, share:width])
             target = op[0][:].rearrange("q (g w) j -> q g w j", g=count)[:, :, 0:share, :]
-            if count == 1 or count % 2 == 0:
-                nc.vector.tensor_copy(
-                    out=target.rearrange("q g (c i) j -> q g c j i", i=RUN),
-                    in_=rows[:, :, :, 0:share].rearrange("q g j (c i) -> q g c j i", i=RUN),
-                )
-            else:
-                nc.vector.tensor_copy(
-                    out=target.rearrange("q g (u w) j -> q u g w j", u=2),
-                    in_=rows[:, :, :, 0:share].rearrange("q g j (u w) -> q u g w j", u=2),
-                )
+            nc.vector.tensor_copy(
+                out=target.rearrange("q g (c i) j -> q g c j i", i=RUN),
+                in_=rows[:, :, :, 0:share].rearrange("q g j (c i) -> q g c j i", i=RUN),
+            )
             done = 0
             step = WIDEST
             while done < count * width:
@@ -104,12 +98,12 @@ def tile_mix_tied_sgd_kernel(tc, x, de, dr, e, p, out):
             return op
 
         def multiply(b, wide, narrow, g, start, stop):
-            cols = slice(g * D + b * D_TILE, g * D + (b + 1) * D_TILE)
+            stationary = slice(g * D + b * D_TILE, g * D + (b + 1) * D_TILE)
             moving = slice(g * H, (g + 1) * H)
             nc.tensor.matmul_mx(
                 out=acc[b][:],
-                lhsT=wide[1][:, cols].bitcast(wide[3]),
-                lhsT_scale=wide[2][:, cols],
+                lhsT=wide[1][:, stationary].bitcast(wide[3]),
+                lhsT_scale=wide[2][:, stationary],
                 rhs=narrow[1][:, moving].bitcast(narrow[3]),
                 rhs_scale=narrow[2][:, moving],
                 start=start,
@@ -161,14 +155,11 @@ def tile_mix_tied_sgd_kernel(tc, x, de, dr, e, p, out):
         round_tile(nc.scalar.copy, 1)
         close(0)
         round_tile(nc.vector.tensor_copy, 2)
-        round_tile(nc.scalar.copy, 3)
-        round_tile(nc.scalar.copy, 4)
-        close(1)
-        close(2)
-        update(0)
-        close(3)
-        update(1)
-        close(4)
-        update(2)
-        update(3)
-        update(4)
+        for b in range(EARLY, D_TILES):
+            round_tile(nc.scalar.copy, b)
+        for b in range(1, EARLY):
+            close(b)
+        for b in range(D_TILES):
+            update(b)
+            if EARLY + b < D_TILES:
+                close(EARLY + b)

@@ -30,6 +30,7 @@ NARROW_SHARE = 272
 LAST_SHARE = 320
 EARLY = 3
 WIDEST = 1024
+DMA_ALIGN = 256
 RUN = 2
 
 
@@ -47,7 +48,7 @@ def tile_mix_tied_sgd_kernel(tc, x, de, dr, e, p, out):
         acc = [psum.tile([P, H], F32, name=f"acc{b}") for b in range(D_TILES)]
 
         def load(pool, tag, source, first, count, cols):
-            rows = pool.tile([P, count, PACK, cols.stop - cols.start], F32, name=tag)
+            rows = pool.tile([P, count, PACK, cols.stop - cols.start], F32, name=tag, align_bytes=DMA_ALIGN)
             nc.sync.dma_start(
                 out=rows[:],
                 in_=source[first * T_PASS : (first + count) * T_PASS, cols].rearrange(
@@ -128,7 +129,7 @@ def tile_mix_tied_sgd_kernel(tc, x, de, dr, e, p, out):
         late = load(keep, "late", dr, LAST, 1, slice(EARLY * D_TILE, D))
         p_rows = p.rearrange("(b q) h -> q b h", q=P)
         o_rows = out.rearrange("(b q) h -> q b h", q=P)
-        p_sb = keep.tile([P, D_TILES, H], F32, name="p_sb")
+        p_sb = keep.tile([P, D_TILES, H], F32, name="p_sb", align_bytes=DMA_ALIGN)
         for b in range(D_TILES):
             nc.sync.dma_start(out=p_sb[:, b : b + 1, :], in_=p_rows[:, b : b + 1, :])
 
@@ -145,7 +146,7 @@ def tile_mix_tied_sgd_kernel(tc, x, de, dr, e, p, out):
             multiply(b, dr_op, e_op, 0, False, True)
 
         def update(b):
-            result = keep.tile([P, H], F32, name=f"result{b}")
+            result = keep.tile([P, H], F32, name=f"result{b}", align_bytes=DMA_ALIGN)
             nc.vector.scalar_tensor_tensor(
                 out=result[:], in0=acc[b][:], scalar=-LEARNING_RATE, in1=p_sb[:, b, :], op0=MULT, op1=ADD
             )

@@ -28,7 +28,7 @@ LAST = PASSES - 1
 WIDE_SHARE = 384
 NARROW_SHARE = 272
 LAST_SHARE = 320
-EARLY = 3
+PIECES = [(0, 2), (2, 2), (4, 1)]
 WIDEST = 1024
 DMA_ALIGN = 256
 RUN = 2
@@ -88,15 +88,20 @@ def tile_mix_tied_sgd_kernel(tc, x, de, dr, e, p, out):
                 out=target.rearrange("q g (c i) j -> q g c j i", i=RUN),
                 in_=rows[:, :, :, 0:share].rearrange("q g j (c i) -> q g c j i", i=RUN),
             )
+            return op
+
+        def calls(op):
+            total = op[1].shape[1]
+            ranges = []
             done = 0
             step = WIDEST
-            while done < count * width:
-                if done + step <= count * width:
-                    quantize(op, slice(done, done + step))
+            while done < total:
+                if done + step <= total:
+                    ranges.append(slice(done, done + step))
                     done = done + step
                 else:
                     step = step // 2
-            return op
+            return ranges
 
         def multiply(b, wide, narrow, g, start, stop):
             stationary = slice(g * D + b * D_TILE, g * D + (b + 1) * D_TILE)
@@ -111,22 +116,40 @@ def tile_mix_tied_sgd_kernel(tc, x, de, dr, e, p, out):
                 stop=stop,
             )
 
+        def finish(wide, narrow, cols):
+            quantize(wide, cols)
+            for tile in range(cols.start // D_TILE, cols.stop // D_TILE):
+                multiply(tile % D_TILES, wide, narrow, tile // D_TILES, False, False)
+
+        pairs = []
         for first, count in GROUPS:
-            for wide_src, wide_fmt, narrow_src, narrow_fmt in ((x, E4M3, de, E5M2), (dr, E5M2, e, E4M3)):
-                narrow = prepare("narrow", narrow_src, narrow_fmt, first, count, NARROW_SHARE)
-                wide = prepare("wide", wide_src, wide_fmt, first, count, WIDE_SHARE)
-                for g in range(count):
-                    for b in range(D_TILES):
-                        multiply(b, wide, narrow, g, first + g == 0 and wide_src is x, False)
+            pairs.append((x, E4M3, de, E5M2, first, count))
+            pairs.append((dr, E5M2, e, E4M3, first, count))
+        pairs.append((x, E4M3, de, E5M2, LAST, 1))
+        held = []
+        for wide_src, wide_fmt, narrow_src, narrow_fmt, first, count in pairs:
+            narrow = prepare("narrow", narrow_src, narrow_fmt, first, count, NARROW_SHARE)
+            for args in held:
+                finish(*args)
+            for cols in calls(narrow):
+                quantize(narrow, cols)
+            wide = prepare("wide", wide_src, wide_fmt, first, count, WIDE_SHARE)
+            ranges = calls(wide)
+            for cols in ranges[:-1]:
+                quantize(wide, cols)
+            for tile in range(ranges[-1].start // D_TILE):
+                opens = first == 0 and wide_src is x and tile < D_TILES
+                multiply(tile % D_TILES, wide, narrow, tile // D_TILES, opens, False)
+            held = [(wide, narrow, ranges[-1])]
 
-        x_op = prepare("wide", x, E4M3, LAST, 1, WIDE_SHARE)
-        de_op = prepare("narrow", de, E5M2, LAST, 1, NARROW_SHARE)
-        for b in range(D_TILES):
-            multiply(b, x_op, de_op, 0, False, False)
         e_op = prepare("narrow", e, E4M3, LAST, 1, LAST_SHARE)
+        finish(*held[0])
 
-        early = load(keep, "early", dr, LAST, 1, slice(0, EARLY * D_TILE))
-        late = load(keep, "late", dr, LAST, 1, slice(EARLY * D_TILE, D))
+        pieces = {}
+        for first, count in PIECES:
+            rows = load(keep, f"piece{first}", dr, LAST, 1, slice(first * D_TILE, (first + count) * D_TILE))
+            for b in range(count):
+                pieces[first + b] = rows[:, 0, :, b * D_TILE : (b + 1) * D_TILE]
         p_rows = p.rearrange("(b q) h -> q b h", q=P)
         o_rows = out.rearrange("(b q) h -> q b h", q=P)
         p_sb = keep.tile([P, D_TILES, H], F32, name="p_sb", align_bytes=DMA_ALIGN)
@@ -136,14 +159,12 @@ def tile_mix_tied_sgd_kernel(tc, x, de, dr, e, p, out):
         dr_op = operand("wide", D, E5M2)
 
         def round_tile(copy, b):
-            rows, place = (early, b) if b < EARLY else (late, b - EARLY)
-            interleave(
-                copy, dr_op, slice(b * D_TILE, (b + 1) * D_TILE), rows[:, 0, :, place * D_TILE : (place + 1) * D_TILE]
-            )
+            interleave(copy, dr_op, slice(b * D_TILE, (b + 1) * D_TILE), pieces[b])
 
-        def close(b):
-            quantize(dr_op, slice(b * D_TILE, (b + 1) * D_TILE))
-            multiply(b, dr_op, e_op, 0, False, True)
+        def close(first, count):
+            quantize(dr_op, slice(first * D_TILE, (first + count) * D_TILE))
+            for b in range(first, first + count):
+                multiply(b, dr_op, e_op, 0, False, True)
 
         def update(b):
             result = keep.tile([P, H], F32, name=f"result{b}", align_bytes=DMA_ALIGN)
@@ -154,13 +175,13 @@ def tile_mix_tied_sgd_kernel(tc, x, de, dr, e, p, out):
 
         round_tile(nc.vector.tensor_copy, 0)
         round_tile(nc.scalar.copy, 1)
-        close(0)
+        quantize(e_op, slice(0, H))
+        close(0, 2)
         round_tile(nc.vector.tensor_copy, 2)
-        for b in range(EARLY, D_TILES):
-            round_tile(nc.scalar.copy, b)
-        for b in range(1, EARLY):
-            close(b)
-        for b in range(D_TILES):
+        round_tile(nc.scalar.copy, 3)
+        round_tile(nc.scalar.copy, 4)
+        close(2, 2)
+        update(0)
+        close(4, 1)
+        for b in range(1, D_TILES):
             update(b)
-            if EARLY + b < D_TILES:
-                close(EARLY + b)

@@ -23,7 +23,9 @@ PASSES = T // T_PASS
 D_TILE = 128
 D_TILES = D // D_TILE
 
-GROUPS = [(0, 3), (3, 2)]
+X_GROUPS = [(0, 5)]
+DR_GROUPS = [(0, 3), (3, 2)]
+PLACES = 3
 LAST = PASSES - 1
 WIDE_SHARE = 384
 NARROW_SHARE = 272
@@ -38,8 +40,8 @@ def tile_mix_tied_sgd_kernel(tc, x, de, dr, e, p, out):
     nc = tc.nc
 
     with ExitStack() as ctx:
-        raw = ctx.enter_context(tc.tile_pool(name="raw", bufs=2))
-        grouped = ctx.enter_context(tc.tile_pool(name="grouped", bufs=2))
+        raw = ctx.enter_context(tc.tile_pool(name="raw", bufs=1))
+        grouped = ctx.enter_context(tc.tile_pool(name="grouped", bufs=1))
         packed = ctx.enter_context(tc.tile_pool(name="packed", bufs=2))
         keep = ctx.enter_context(tc.tile_pool(name="keep", bufs=1))
         psum = ctx.enter_context(tc.psum_pool(name="psum", bufs=1))
@@ -57,8 +59,8 @@ def tile_mix_tied_sgd_kernel(tc, x, de, dr, e, p, out):
             )
             return rows
 
-        def operand(tag, width, fmt):
-            values = grouped.tile([P, width, PACK], BF16, name=tag + "_grp", align_bytes=64)
+        def operand(tag, width, fmt, values_tag):
+            values = grouped.tile([P, width, PACK], BF16, name=values_tag, align_bytes=64)
             codes = packed.tile([P, width], U32, name=tag + "_codes", align_bytes=64)
             scales = packed.tile([P, width], U8, name=tag + "_scales", align_bytes=64)
             return values, codes, scales, fmt
@@ -77,17 +79,19 @@ def tile_mix_tied_sgd_kernel(tc, x, de, dr, e, p, out):
                 in_=values[:, cols, :].rearrange("q w j -> q (w j)"),
             )
 
+        loads = []
+
         def prepare(tag, source, fmt, first, count, share):
             width = source.shape[1]
-            rows = load(raw, tag + "_raw", source, first, count, slice(0, width))
-            op = operand(tag, count * width, fmt)
-            for g in range(count):
-                interleave(nc.scalar.copy, op, slice(g * width + share, (g + 1) * width), rows[:, g, :, share:width])
-            target = op[0][:].rearrange("q (g w) j -> q g w j", g=count)[:, :, 0:share, :]
-            nc.vector.tensor_copy(
-                out=target.rearrange("q g (c i) j -> q g c j i", i=RUN),
-                in_=rows[:, :, :, 0:share].rearrange("q g j (c i) -> q g c j i", i=RUN),
-            )
+            rows = load(raw, f"place{len(loads) % PLACES}", source, first, count, slice(0, width))
+            loads.append(rows)
+            op = operand(tag, count * width, fmt, tag + "_grp")
+            target = op[0][:].rearrange("q (g w) j -> q g w j", g=count)
+            for copy, cols in ((nc.scalar.copy, slice(share, width)), (nc.vector.tensor_copy, slice(0, share))):
+                copy(
+                    out=target[:, :, cols, :].rearrange("q g (c i) j -> q g c j i", i=RUN),
+                    in_=rows[:, :, :, cols].rearrange("q g j (c i) -> q g c j i", i=RUN),
+                )
             return op
 
         def calls(op):
@@ -116,34 +120,32 @@ def tile_mix_tied_sgd_kernel(tc, x, de, dr, e, p, out):
                 stop=stop,
             )
 
-        def finish(wide, narrow, cols):
-            quantize(wide, cols)
-            for tile in range(cols.start // D_TILE, cols.stop // D_TILE):
-                multiply(tile % D_TILES, wide, narrow, tile // D_TILES, False, False)
+        def advance(wide, narrow, ranges, opening):
+            for cols in ranges:
+                quantize(wide, cols)
+            for cols in ranges:
+                for tile in range(cols.start // D_TILE, cols.stop // D_TILE):
+                    multiply(tile % D_TILES, wide, narrow, tile // D_TILES, opening and tile < D_TILES, False)
 
         pairs = []
-        for first, count in GROUPS:
+        for first, count in X_GROUPS:
             pairs.append((x, E4M3, de, E5M2, first, count))
+        for first, count in DR_GROUPS:
             pairs.append((dr, E5M2, e, E4M3, first, count))
         pairs.append((x, E4M3, de, E5M2, LAST, 1))
         held = []
         for wide_src, wide_fmt, narrow_src, narrow_fmt, first, count in pairs:
             narrow = prepare("narrow", narrow_src, narrow_fmt, first, count, NARROW_SHARE)
             for args in held:
-                finish(*args)
+                advance(*args)
             for cols in calls(narrow):
                 quantize(narrow, cols)
             wide = prepare("wide", wide_src, wide_fmt, first, count, WIDE_SHARE)
-            ranges = calls(wide)
-            for cols in ranges[:-1]:
-                quantize(wide, cols)
-            for tile in range(ranges[-1].start // D_TILE):
-                opens = first == 0 and wide_src is x and tile < D_TILES
-                multiply(tile % D_TILES, wide, narrow, tile // D_TILES, opens, False)
-            held = [(wide, narrow, ranges[-1])]
+            held = [(wide, narrow, calls(wide), not held)]
 
+        advance(wide, narrow, calls(wide)[:-1], False)
         e_op = prepare("narrow", e, E4M3, LAST, 1, LAST_SHARE)
-        finish(*held[0])
+        advance(wide, narrow, calls(wide)[-1:], False)
 
         pieces = {}
         for first, count in PIECES:
@@ -152,11 +154,12 @@ def tile_mix_tied_sgd_kernel(tc, x, de, dr, e, p, out):
                 pieces[first + b] = rows[:, 0, :, b * D_TILE : (b + 1) * D_TILE]
         p_rows = p.rearrange("(b q) h -> q b h", q=P)
         o_rows = out.rearrange("(b q) h -> q b h", q=P)
-        p_sb = keep.tile([P, D_TILES, H], F32, name="p_sb", align_bytes=DMA_ALIGN)
+        p_sb = raw.tile([P, D_TILES, H], F32, name=f"place{len(loads) % PLACES}", align_bytes=DMA_ALIGN)
+        results = raw.tile([P, D_TILES, H], F32, name=f"place{(len(loads) + 1) % PLACES}", align_bytes=DMA_ALIGN)
         for b in range(D_TILES):
             nc.sync.dma_start(out=p_sb[:, b : b + 1, :], in_=p_rows[:, b : b + 1, :])
 
-        dr_op = operand("wide", D, E5M2)
+        dr_op = operand("wide", D, E5M2, "last_grp")
 
         def round_tile(copy, b):
             interleave(copy, dr_op, slice(b * D_TILE, (b + 1) * D_TILE), pieces[b])
@@ -167,11 +170,10 @@ def tile_mix_tied_sgd_kernel(tc, x, de, dr, e, p, out):
                 multiply(b, dr_op, e_op, 0, False, True)
 
         def update(b):
-            result = keep.tile([P, H], F32, name=f"result{b}", align_bytes=DMA_ALIGN)
             nc.vector.scalar_tensor_tensor(
-                out=result[:], in0=acc[b][:], scalar=-LEARNING_RATE, in1=p_sb[:, b, :], op0=MULT, op1=ADD
+                out=results[:, b, :], in0=acc[b][:], scalar=-LEARNING_RATE, in1=p_sb[:, b, :], op0=MULT, op1=ADD
             )
-            nc.sync.dma_start(out=o_rows[:, b, :], in_=result[:])
+            nc.sync.dma_start(out=o_rows[:, b, :], in_=results[:, b, :])
 
         round_tile(nc.vector.tensor_copy, 0)
         round_tile(nc.scalar.copy, 1)

@@ -156,8 +156,11 @@ def tile_mix_tied_sgd_kernel(tc, x, de, dr, e, p, out):
         o_rows = out.rearrange("(b q) h -> q b h", q=P)
         p_sb = raw.tile([P, D_TILES, H], F32, name=f"place{len(loads) % PLACES}", align_bytes=DMA_ALIGN)
         results = raw.tile([P, D_TILES, H], F32, name=f"place{(len(loads) + 1) % PLACES}", align_bytes=DMA_ALIGN)
-        for b in range(D_TILES):
-            nc.sync.dma_start(out=p_sb[:, b : b + 1, :], in_=p_rows[:, b : b + 1, :])
+        parts = [(b, slice(0, H)) for b in range(D_TILES - 1)]
+        parts.append((D_TILES - 1, slice(0, H // 2)))
+        parts.append((D_TILES - 1, slice(H // 2, H)))
+        for b, cols in parts:
+            nc.sync.dma_start(out=p_sb[:, b, cols], in_=p_rows[:, b, cols])
 
         dr_op = operand("wide", D, E5M2, "last_grp")
 
@@ -169,11 +172,14 @@ def tile_mix_tied_sgd_kernel(tc, x, de, dr, e, p, out):
             for b in range(first, first + count):
                 multiply(b, dr_op, e_op, 0, False, True)
 
-        def update(b):
+        def update(b, cols, queue):
             nc.vector.scalar_tensor_tensor(
-                out=results[:, b, :], in0=acc[b][:], scalar=-LEARNING_RATE, in1=p_sb[:, b, :], op0=MULT, op1=ADD
+                out=results[:, b, cols], in0=acc[b][:, cols], scalar=-LEARNING_RATE, in1=p_sb[:, b, cols],
+                op0=MULT, op1=ADD,
             )
-            nc.sync.dma_start(out=o_rows[:, b, :], in_=results[:, b, :])
+            queue.dma_start(out=o_rows[:, b, cols], in_=results[:, b, cols])
+
+        queues = (nc.scalar, nc.sync)
 
         round_tile(nc.vector.tensor_copy, 0)
         round_tile(nc.scalar.copy, 1)
@@ -183,7 +189,7 @@ def tile_mix_tied_sgd_kernel(tc, x, de, dr, e, p, out):
         round_tile(nc.scalar.copy, 3)
         round_tile(nc.scalar.copy, 4)
         close(2, 2)
-        update(0)
+        update(*parts[0], queues[0])
         close(4, 1)
-        for b in range(1, D_TILES):
-            update(b)
+        for i in range(1, len(parts)):
+            update(*parts[i], queues[i % 2])

@@ -15,6 +15,7 @@ E4M3 = mybir.dt.float8_e4m3fn_x4
 E5M2 = mybir.dt.float8_e5m2_x4
 MULT = mybir.AluOpType.mult
 ADD = mybir.AluOpType.add
+COPY = mybir.ActivationFunctionType.Copy
 
 P = 128
 PACK = 4
@@ -33,6 +34,7 @@ LAST_SHARE = 320
 PIECES = [(0, 2), (2, 2), (4, 1)]
 WIDEST = 1024
 DMA_ALIGN = 256
+POOL_SHARE = 192
 RUN = 2
 
 
@@ -172,6 +174,18 @@ def tile_mix_tied_sgd_kernel(tc, x, de, dr, e, p, out):
             for b in range(first, first + count):
                 multiply(b, dr_op, e_op, 0, False, True)
 
+        steps = keep.tile([P, D_TILES, POOL_SHARE], F32, name="steps", align_bytes=64)
+
+        def update_shared(b, cols, queue):
+            first, rest = slice(0, POOL_SHARE), slice(POOL_SHARE, H)
+            nc.scalar.activation(out=steps[:, b, :], in_=acc[b][:, first], func=COPY, scale=-LEARNING_RATE)
+            nc.gpsimd.tensor_tensor(out=results[:, b, first], in0=steps[:, b, :], in1=p_sb[:, b, first], op=ADD)
+            nc.vector.scalar_tensor_tensor(
+                out=results[:, b, rest], in0=acc[b][:, rest], scalar=-LEARNING_RATE, in1=p_sb[:, b, rest],
+                op0=MULT, op1=ADD,
+            )
+            nc.sync.dma_start(out=o_rows[:, b, cols], in_=results[:, b, cols])
+
         def update(b, cols, queue):
             nc.vector.scalar_tensor_tensor(
                 out=results[:, b, cols], in0=acc[b][:, cols], scalar=-LEARNING_RATE, in1=p_sb[:, b, cols],
@@ -189,7 +203,9 @@ def tile_mix_tied_sgd_kernel(tc, x, de, dr, e, p, out):
         round_tile(nc.scalar.copy, 3)
         round_tile(nc.scalar.copy, 4)
         close(2, 2)
-        update(*parts[0], queues[0])
+        update(*parts[0], nc.sync)
         close(4, 1)
-        for i in range(1, len(parts)):
-            update(*parts[i], queues[i % 2])
+        for i in range(1, 4):
+            update_shared(*parts[i], nc.sync)
+        update(*parts[4], nc.scalar)
+        update(*parts[5], nc.sync)

@@ -34,7 +34,7 @@ LAST_SHARE = 320
 PIECES = [(0, 2), (2, 2), (4, 1)]
 WIDEST = 1024
 DMA_ALIGN = 256
-POOL_SHARE = 192
+POOL_SHARE = 128
 RUN = 2
 
 
@@ -89,10 +89,14 @@ def tile_mix_tied_sgd_kernel(tc, x, de, dr, e, p, out):
             loads.append(rows)
             op = operand(tag, count * width, fmt, tag + "_grp")
             target = op[0][:].rearrange("q (g w) j -> q g w j", g=count)
-            for copy, cols in ((nc.scalar.copy, slice(share, width)), (nc.vector.tensor_copy, slice(0, share))):
+            walk = "q c g j i" if count % 2 else "q g c j i"
+            for copy, cols, order in (
+                (nc.scalar.copy, slice(share, width), "q g c j i"),
+                (nc.vector.tensor_copy, slice(0, share), walk),
+            ):
                 copy(
-                    out=target[:, :, cols, :].rearrange("q g (c i) j -> q g c j i", i=RUN),
-                    in_=rows[:, :, :, cols].rearrange("q g j (c i) -> q g c j i", i=RUN),
+                    out=target[:, :, cols, :].rearrange("q g (c i) j -> " + order, i=RUN),
+                    in_=rows[:, :, :, cols].rearrange("q g j (c i) -> " + order, i=RUN),
                 )
             return op
 
@@ -161,8 +165,8 @@ def tile_mix_tied_sgd_kernel(tc, x, de, dr, e, p, out):
         parts = [(b, slice(0, H)) for b in range(D_TILES - 1)]
         parts.append((D_TILES - 1, slice(0, H // 2)))
         parts.append((D_TILES - 1, slice(H // 2, H)))
-        for b, cols in parts:
-            nc.sync.dma_start(out=p_sb[:, b, cols], in_=p_rows[:, b, cols])
+        for b in range(D_TILES):
+            nc.sync.dma_start(out=p_sb[:, b, :], in_=p_rows[:, b, :])
 
         dr_op = operand("wide", D, E5M2, "last_grp")
 
@@ -203,9 +207,11 @@ def tile_mix_tied_sgd_kernel(tc, x, de, dr, e, p, out):
         round_tile(nc.scalar.copy, 3)
         round_tile(nc.scalar.copy, 4)
         close(2, 2)
-        update(*parts[0], nc.sync)
+        update(0, slice(0, H // 2), nc.sync)
+        update(0, slice(H // 2, H), nc.sync)
+        update_shared(*parts[1], nc.sync)
         close(4, 1)
-        for i in range(1, 4):
+        for i in range(2, 4):
             update_shared(*parts[i], nc.sync)
         update(*parts[4], nc.scalar)
         update(*parts[5], nc.sync)

@@ -211,7 +211,7 @@ def tile_mix_tied_sgd_kernel(tc, x, de, dr, e, p, out):
         update(0, slice(H // 2, H), nc.sync)
         update_shared(*parts[1], nc.sync)
         close(4, 1)
-        for i in range(2, 4):
-            update_shared(*parts[i], nc.sync)
+        update_shared(*parts[2], nc.sync)
+        update(*parts[3], nc.sync)
         update(*parts[4], nc.scalar)
         update(*parts[5], nc.sync)

from contextlib import ExitStack

import concourse.mybir as mybir

T, D, H = 3072, 640, 512
LEARNING_RATE = 0.0625

FLOPS = 4 * T * D * H

F32 = mybir.dt.float32
BF16 = mybir.dt.bfloat16
U32 = mybir.dt.uint32
U8 = mybir.dt.uint8
E4M3 = mybir.dt.float8_e4m3fn_x4
E5M2 = mybir.dt.float8_e5m2_x4
MULT = mybir.AluOpType.mult
ADD = mybir.AluOpType.add
COPY = mybir.ActivationFunctionType.Copy

P = 128
PACK = 4
T_PASS = P * PACK
PASSES = T // T_PASS
D_TILE = 128
D_TILES = D // D_TILE

X_GROUPS = [(0, 5)]
DR_GROUPS = [(0, 3), (3, 2)]
PLACES = 3
LAST = PASSES - 1
WIDE_SHARE = 384
NARROW_SHARE = 272
LAST_SHARE = 320
PIECES = [(0, 2), (2, 2), (4, 1)]
WIDEST = 1024
DMA_ALIGN = 256
POOL_SHARE = 128
RUN = 2


def tile_mix_tied_sgd_kernel(tc, x, de, dr, e, p, out):
    nc = tc.nc

    with ExitStack() as ctx:
        raw = ctx.enter_context(tc.tile_pool(name="raw", bufs=1))
        grouped = ctx.enter_context(tc.tile_pool(name="grouped", bufs=1))
        packed = ctx.enter_context(tc.tile_pool(name="packed", bufs=2))
        keep = ctx.enter_context(tc.tile_pool(name="keep", bufs=1))
        psum = ctx.enter_context(tc.psum_pool(name="psum", bufs=1))
        ctx.enter_context(tc.manual_schedule())

        acc = [psum.tile([P, H], F32, name=f"acc{b}") for b in range(D_TILES)]

        def load(pool, tag, source, first, count, cols):
            rows = pool.tile([P, count, PACK, cols.stop - cols.start], F32, name=tag, align_bytes=DMA_ALIGN)
            nc.sync.dma_start(
                out=rows[:],
                in_=source[first * T_PASS : (first + count) * T_PASS, cols].rearrange(
                    "(g q j) w -> q g j w", g=count, j=PACK
                ),
            )
            return rows

        def operand(tag, width, fmt, values_tag):
            values = grouped.tile([P, width, PACK], BF16, name=values_tag, align_bytes=64)
            codes = packed.tile([P, width], U32, name=tag + "_codes", align_bytes=64)
            scales = packed.tile([P, width], U8, name=tag + "_scales", align_bytes=64)
            return values, codes, scales, fmt

        def interleave(copy, op, cols, rows):
            copy(
                out=op[0][:, cols, :].rearrange("q (c i) j -> q c j i", i=RUN),
                in_=rows.rearrange("q j (c i) -> q c j i", i=RUN),
            )

        def quantize(op, cols):
            values, codes, scales, fmt = op
            nc.vector.quantize_mx(
                out=codes[:, cols].bitcast(fmt),
                scales=scales[:, cols],
                in_=values[:, cols, :].rearrange("q w j -> q (w j)"),
            )

        loads = []

        def prepare(tag, source, fmt, first, count, share):
            width = source.shape[1]
            rows = load(raw, f"place{len(loads) % PLACES}", source, first, count, slice(0, width))
            loads.append(rows)
            op = operand(tag, count * width, fmt, tag + "_grp")
            target = op[0][:].rearrange("q (g w) j -> q g w j", g=count)
            walk = "q c g j i" if count % 2 else "q g c j i"
            for copy, cols, order in (
                (nc.scalar.copy, slice(share, width), "q g c j i"),
                (nc.vector.tensor_copy, slice(0, share), walk),
            ):
                copy(
                    out=target[:, :, cols, :].rearrange("q g (c i) j -> " + order, i=RUN),
                    in_=rows[:, :, :, cols].rearrange("q g j (c i) -> " + order, i=RUN),
                )
            return op

        def calls(op):
            total = op[1].shape[1]
            ranges = []
            done = 0
            step = WIDEST
            while done < total:
                if done + step <= total:
                    ranges.append(slice(done, done + step))
                    done = done + step
                else:
                    step = step // 2
            return ranges

        def multiply(b, wide, narrow, g, start, stop):
            stationary = slice(g * D + b * D_TILE, g * D + (b + 1) * D_TILE)
            moving = slice(g * H, (g + 1) * H)
            nc.tensor.matmul_mx(
                out=acc[b][:],
                lhsT=wide[1][:, stationary].bitcast(wide[3]),
                lhsT_scale=wide[2][:, stationary],
                rhs=narrow[1][:, moving].bitcast(narrow[3]),
                rhs_scale=narrow[2][:, moving],
                start=start,
                stop=stop,
            )

        def advance(wide, narrow, ranges, opening):
            for cols in ranges:
                quantize(wide, cols)
            for cols in ranges:
                for tile in range(cols.start // D_TILE, cols.stop // D_TILE):
                    multiply(tile % D_TILES, wide, narrow, tile // D_TILES, opening and tile < D_TILES, False)

        pairs = []
        for first, count in X_GROUPS:
            pairs.append((x, E4M3, de, E5M2, first, count))
        for first, count in DR_GROUPS:
            pairs.append((dr, E5M2, e, E4M3, first, count))
        pairs.append((x, E4M3, de, E5M2, LAST, 1))
        held = []
        for wide_src, wide_fmt, narrow_src, narrow_fmt, first, count in pairs:
            narrow = prepare("narrow", narrow_src, narrow_fmt, first, count, NARROW_SHARE)
            for args in held:
                advance(*args)
            for cols in calls(narrow):
                quantize(narrow, cols)
            wide = prepare("wide", wide_src, wide_fmt, first, count, WIDE_SHARE)
            held = [(wide, narrow, calls(wide), not held)]

        advance(wide, narrow, calls(wide)[:-1], False)
        e_op = prepare("narrow", e, E4M3, LAST, 1, LAST_SHARE)
        advance(wide, narrow, calls(wide)[-1:], False)

        pieces = {}
        for first, count in PIECES:
            rows = load(keep, f"piece{first}", dr, LAST, 1, slice(first * D_TILE, (first + count) * D_TILE))
            for b in range(count):
                pieces[first + b] = rows[:, 0, :, b * D_TILE : (b + 1) * D_TILE]
        p_rows = p.rearrange("(b q) h -> q b h", q=P)
        o_rows = out.rearrange("(b q) h -> q b h", q=P)
        p_sb = raw.tile([P, D_TILES, H], F32, name=f"place{len(loads) % PLACES}", align_bytes=DMA_ALIGN)
        results = raw.tile([P, D_TILES, H], F32, name=f"place{(len(loads) + 1) % PLACES}", align_bytes=DMA_ALIGN)
        parts = [(b, slice(0, H)) for b in range(D_TILES - 1)]
        parts.append((D_TILES - 1, slice(0, H // 2)))
        parts.append((D_TILES - 1, slice(H // 2, H)))
        for b in range(D_TILES):
            nc.sync.dma_start(out=p_sb[:, b, :], in_=p_rows[:, b, :])

        dr_op = operand("wide", D, E5M2, "last_grp")

        def round_tile(copy, b):
            interleave(copy, dr_op, slice(b * D_TILE, (b + 1) * D_TILE), pieces[b])

        def close(first, count):
            quantize(dr_op, slice(first * D_TILE, (first + count) * D_TILE))
            for b in range(first, first + count):
                multiply(b, dr_op, e_op, 0, False, True)

        steps = keep.tile([P, D_TILES, POOL_SHARE], F32, name="steps", align_bytes=64)

        def update_shared(b, cols, queue):
            first, rest = slice(0, POOL_SHARE), slice(POOL_SHARE, H)
            nc.scalar.activation(out=steps[:, b, :], in_=acc[b][:, first], func=COPY, scale=-LEARNING_RATE)
            nc.gpsimd.tensor_tensor(out=results[:, b, first], in0=steps[:, b, :], in1=p_sb[:, b, first], op=ADD)
            nc.vector.scalar_tensor_tensor(
                out=results[:, b, rest], in0=acc[b][:, rest], scalar=-LEARNING_RATE, in1=p_sb[:, b, rest],
                op0=MULT, op1=ADD,
            )
            nc.sync.dma_start(out=o_rows[:, b, cols], in_=results[:, b, cols])

        def update(b, cols, queue):
            nc.vector.scalar_tensor_tensor(
                out=results[:, b, cols], in0=acc[b][:, cols], scalar=-LEARNING_RATE, in1=p_sb[:, b, cols],
                op0=MULT, op1=ADD,
            )
            queue.dma_start(out=o_rows[:, b, cols], in_=results[:, b, cols])

        queues = (nc.scalar, nc.sync)

        round_tile(nc.vector.tensor_copy, 0)
        round_tile(nc.scalar.copy, 1)
        quantize(e_op, slice(0, H))
        close(0, 2)
        round_tile(nc.vector.tensor_copy, 2)
        round_tile(nc.scalar.copy, 3)
        round_tile(nc.scalar.copy, 4)
        close(2, 2)
        update(0, slice(0, H // 2), nc.sync)
        update(0, slice(H // 2, H), nc.sync)
        update_shared(*parts[1], nc.sync)
        close(4, 1)
        update_shared(*parts[2], nc.sync)
        update(*parts[3], nc.sync)
        update(*parts[4], nc.scalar)
        update(*parts[5], nc.sync)
